import numpy as np
import ml_dtypes


def mxq(x, axis, fmt="e4m3"):
    dtype, down = {"e4m3": (ml_dtypes.float8_e4m3fn, 7), "e5m2": (ml_dtypes.float8_e5m2, 14)}[fmt]
    v = np.moveaxis(np.asarray(x, np.float32).astype(ml_dtypes.bfloat16).astype(np.float64), axis, -1)
    blocks = v.reshape(v.shape[:-1] + (-1, 32))
    amax = np.abs(blocks).max(-1, keepdims=True)
    byte = np.maximum(np.where(amax > 0, np.frexp(amax)[1] - 1 + 127, 0) - down, 1)
    scale = np.exp2(byte - 127.0)
    codes = (blocks / scale).astype(np.float32).astype(dtype).astype(np.float64)
    return np.moveaxis((codes * scale).reshape(v.shape), -1, axis)


WIDE = False


def mx_kscale(k):
    if not WIDE:
        return np.ones(k)
    levels = np.array([10, -10, 5, -5, 0])
    if k % 512:
        return np.exp2(np.random.permutation(np.resize(levels, k // 32))).repeat(32)
    a = np.empty((k // 512, 16))
    for p in range(k // 512):
        a[p, :8] = np.random.permutation(np.resize(levels, 8))
        for g in range(8):
            far = levels[np.abs(levels - a[p, g]) >= 10]
            a[p, g + 8] = far[np.random.randint(len(far))]
    return np.exp2(a.ravel()).repeat(32)


def f64(x):
    return np.asarray(x).astype(np.float64)


def striped(idx):
    return np.tile(idx.reshape(-1, 16).T, (8, 1)).astype(np.uint16)


def unstriped(offs):
    return offs[:16].T.reshape(-1).astype(np.int64)


def pack_weight(w):
    k, n = w.shape
    w = f64(np.asarray(w, np.float32).astype(ml_dtypes.bfloat16)).reshape(k // 32, 32, n)
    amax = np.abs(w).max(1)
    byte = np.clip(np.where(amax > 0, np.frexp(amax)[1] - 1 + 127 - 7, 1), 1, 254)
    scaled = (w * np.exp2(127.0 - byte)[:, None, :]).reshape(k, n).astype(np.float32)
    words = np.ascontiguousarray(scaled.reshape(k // 512, 128, 4, n).transpose(0, 1, 3, 2)).astype(ml_dtypes.float8_e4m3fn).view(np.uint8)
    return words, np.ascontiguousarray(byte.astype(np.uint8).reshape(k // 512, 16, n))


def unpack_weight(words, scales):
    g, p, n, _ = words.shape
    vals = np.ascontiguousarray(words).view(ml_dtypes.float8_e4m3fn).astype(np.float64) * np.repeat(np.exp2(scales.astype(np.float64) - 127.0), 8, axis=1)[..., None]
    return vals.transpose(0, 1, 3, 2).reshape(g * 512, n)


K, T, S, N, G, H, U = 512, 2048, 256, 512, 2048, 512, 512


def setup_inputs():
    n = np.random.standard_normal
    s = mx_kscale(K)[:, None]
    u = mx_kscale(K)
    packed_xT = pack_weight(n((K, T)) * s)
    packed_dT = pack_weight(n((K, G)) / s)
    perm = np.random.permutation(U)
    return {
        "x_words": packed_xT[0],
        "x_scales": packed_xT[1],
        "d_words": packed_dT[0],
        "d_scales": packed_dT[1],
        "gn": (np.random.uniform(0.5, 1.5, (H, 1)) * u[:, None]).astype(np.float32),
        "w1": (n((H, N)) / np.sqrt(H) / u[:, None]).astype(np.float32),
        "offs": striped(np.random.permutation(T)[:S]),
        "ci": striped(np.random.permutation(G)[:H]),
        "n1": striped(perm[:S]),
        "n2": striped(perm[S:]),
        "n3": striped(np.random.permutation(U)),
    }


def reference(x_words, x_scales, d_words, d_scales, gn, w1, offs, ci, n1, n2, n3):
    d_ci = unpack_weight(d_words, d_scales)[:, unstriped(ci)]
    xq = unpack_weight(x_words, x_scales)[:, unstriped(offs)]
    s = 0.0625 * (d_ci.T @ xq)
    z = f64(gn) * s
    h = mxq(f64(w1), 0, "e4m3").T @ mxq(z, 0, "e4m3")
    nw = 0.5 * h
    ph = np.zeros((N, U))
    ph[:, unstriped(n1)] = h
    pg = ph.copy()
    pg[:, unstriped(n2)] = nw
    return pg - pg[:, unstriped(n3)]

@@ -1,0 +1,186 @@
+from contextlib import ExitStack
+
+import concourse.mybir as mybir
+
+F32 = mybir.dt.float32
+BF16 = mybir.dt.bfloat16
+I32 = mybir.dt.int32
+U32 = mybir.dt.uint32
+U16 = mybir.dt.uint16
+U8 = mybir.dt.uint8
+FP8X4 = mybir.dt.float8_e4m3fn_x4
+MULT = mybir.AluOpType.mult
+SUBTRACT = mybir.AluOpType.subtract
+COPY = mybir.ActivationFunctionType.Copy
+
+P = 128
+PACK = 4
+TABLE = 2048
+S = 256
+H = 512
+N = 512
+U = 512
+HALF = S // 2
+X_ROW = 4
+
+FLOPS = 2 * 512 * H * S + 2 * H * N * S
+
+
+def tile_picked_dwlipagtwo_none_p_kernel(
+    tc, x_words, x_scales, d_words, d_scales, gn, w1, offs, ci, n1, n2, n3, out
+):
+    nc = tc.nc
+    with ExitStack() as ctx:
+        lists = ctx.enter_context(tc.tile_pool(name="lists", bufs=1))
+        keep = ctx.enter_context(tc.tile_pool(name="keep", bufs=1))
+        psum = ctx.enter_context(tc.psum_pool(name="psum", bufs=1))
+
+        def load_list(name, src):
+            t = lists.tile([P, src.shape[1]], U16, name=name)
+            nc.sync.dma_start(t[:], src)
+            return t
+
+        def load_scales(name, src, row):
+            t = keep.tile([P, TABLE], U8, name=name)
+            nc.vector.memset(t[:].bitcast(I32), 0)
+            for q in range(4):
+                nc.scalar.dma_start(
+                    out=t[32 * q + row : 32 * q + row + 4, :].bitcast(I32),
+                    in_=src[0, 4 * q : 4 * q + 4, :].bitcast(I32),
+                )
+            return t
+
+        def load_words(name, src):
+            t = keep.tile([P, TABLE], U32, name=name)
+            nc.sync.dma_start(out=t[:].bitcast(I32), in_=src[0].rearrange("p c r -> p (c r)").bitcast(I32))
+            return t
+
+        ci_t = load_list("ci_t", ci)
+        offs_t = load_list("offs_t", offs)
+        d_scale_table = load_scales("d_scale_table", d_scales, 0)
+        d_word_table = load_words("d_word_table", d_words)
+        x_word_table = load_words("x_word_table", x_words)
+        x_scale_table = load_scales("x_scale_table", x_scales, X_ROW)
+
+        w_rows = w1.rearrange("(p t) m -> p t m", t=PACK)
+        w_first = keep.tile([P, PACK, P], F32)
+        nc.sync.dma_start(out=w_first[:], in_=w_rows[:, :, 0:P])
+        gain = keep.tile([P, PACK], F32)
+        nc.sync.dma_start(out=gain[:], in_=gn.rearrange("(p t) o -> p (t o)", t=PACK))
+        n1_t = load_list("n1_t", n1)
+        n2_t = load_list("n2_t", n2)
+        w_rest = keep.tile([P, PACK, N - P], F32)
+        nc.sync.dma_start(out=w_rest[:], in_=w_rows[:, :, P:N])
+        n3_t = load_list("n3_t", n3)
+
+        d_scale = keep.tile([P, PACK, P], U8, align_bytes=64)
+        nc.vector.tensor_copy(d_scale[:].rearrange("p t s -> p s t"), d_scale_table[:].indirect(ci_t[:]))
+        x_scale = keep.tile([P, S], U8, align_bytes=64)
+        nc.vector.tensor_copy(x_scale[:], x_scale_table[:].indirect(offs_t[:]))
+        d_code = keep.tile([P, PACK, P], U32, align_bytes=64)
+        nc.vector.tensor_copy(d_code[:].rearrange("p t s -> p s t"), d_word_table[:].indirect(ci_t[:]))
+
+        score = []
+        for a in range(2):
+            x_code = keep.tile([P, HALF], U32, align_bytes=64, name=f"x_code{a}")
+            nc.vector.tensor_copy(x_code[:], x_word_table[:].indirect(offs_t[:, 8 * a : 8 * a + 8]))
+            bank = psum.tile([P, PACK, HALF], F32, name=f"score{a}")
+            for t in range(PACK):
+                nc.tensor.matmul_mx(
+                    out=bank[:, t, :],
+                    lhsT=d_code[:, t, :].bitcast(FP8X4),
+                    lhsT_scale=d_scale[:, t, :],
+                    rhs=x_code[:].bitcast(FP8X4),
+                    rhs_scale=x_scale[X_ROW:P, a * HALF : (a + 1) * HALF],
+                    start=True,
+                    stop=True,
+                )
+            score.append(bank)
+
+        def round_weights(b, copy):
+            raw = w_first[:] if b == 0 else w_rest[:, :, (b - 1) * P : b * P]
+            grouped = keep.tile([P, P, PACK], BF16, align_bytes=64, name=f"w_bf{b}")
+            copy(grouped[:].rearrange("p (c i) t -> p c t i", i=4), raw.rearrange("p t (c i) -> p c t i", i=4))
+            return grouped
+
+        def quantise_weights(b, grouped):
+            code = keep.tile([P, P], U32, align_bytes=64, name=f"w_code{b}")
+            scale = keep.tile([P, P], U8, align_bytes=64, name=f"w_scale{b}")
+            nc.vector.quantize_mx(out=code[:].bitcast(FP8X4), scales=scale[:], in_=grouped[:].rearrange("p c t -> p (c t)"))
+            return code, scale
+
+        w_bf0 = round_weights(0, nc.scalar.copy)
+
+        z_code = keep.tile([P, S], U32, align_bytes=64)
+        z_scale = keep.tile([P, S], U8, align_bytes=64)
+        z_bf = []
+        for a in range(2):
+            t = keep.tile([P, HALF, PACK], BF16, align_bytes=64, name=f"z_bf{a}")
+            nc.vector.scalar_tensor_tensor(
+                out=t[:],
+                in0=score[a][:].rearrange("p t j -> p j t"),
+                scalar=0.0625,
+                in1=gain[:].unsqueeze(1).to_broadcast([P, HALF, PACK]),
+                op0=MULT,
+                op1=MULT,
+            )
+            z_bf.append(t)
+
+        def quantise_z(a):
+            cols = slice(a * HALF, (a + 1) * HALF)
+            nc.vector.quantize_mx(out=z_code[:, cols].bitcast(FP8X4), scales=z_scale[:, cols], in_=z_bf[a][:].rearrange("p j t -> p (j t)"))
+
+        h_sb = [keep.tile([P, S], F32, name=f"h{b}") for b in range(4)]
+        page = [keep.tile([P, U], F32, name=f"page{b}") for b in range(4)]
+
+        def layer(b, w, lo, hi):
+            bank = psum.tile([P, hi - lo], F32, name=f"h_bank{b}_{lo}")
+            nc.tensor.matmul_mx(
+                out=bank[:],
+                lhsT=w[0][:].bitcast(FP8X4),
+                lhsT_scale=w[1][:],
+                rhs=z_code[:, lo:hi].bitcast(FP8X4),
+                rhs_scale=z_scale[:, lo:hi],
+                start=True,
+                stop=True,
+            )
+            nc.vector.tensor_copy(h_sb[b][:, lo:hi], bank[:])
+
+        def put(b, which, lo, hi):
+            idx, factor = ((n1_t, 1.0), (n2_t, 0.5))[which]
+            nc.scalar.activation(page[b][:].indirect(idx[:, lo // 16 : hi // 16]), h_sb[b][:, lo:hi], COPY, scale=factor)
+
+        def fetch(b, lo, hi):
+            got = keep.tile([P, hi - lo], F32, name=f"got{b}_{lo}")
+            nc.scalar.activation(got[:], page[b][:].indirect(n3_t[:, lo // 16 : hi // 16]), COPY)
+            res = keep.tile([P, hi - lo], F32, name=f"res{b}_{lo}")
+            nc.vector.tensor_tensor(res[:], page[b][:, lo:hi], got[:], SUBTRACT)
+            nc.sync.dma_start(out=out[b * P : (b + 1) * P, lo:hi], in_=res[:])
+
+        quantise_z(0)
+        w0 = quantise_weights(0, w_bf0)
+        quantise_z(1)
+        layer(0, w0, 0, HALF)
+        layer(0, w0, HALF, S)
+        for b in range(1, 4):
+            layer(b, quantise_weights(b, round_weights(b, nc.vector.tensor_copy)), 0, S)
+
+        put(0, 0, 0, HALF)
+        put(0, 1, 0, HALF)
+        put(0, 0, HALF, S)
+        put(1, 0, 0, S)
+        put(0, 1, HALF, S)
+        put(1, 1, 0, S)
+        fetch(0, 0, 256)
+        fetch(0, 256, 512)
+        put(2, 0, 0, S)
+        fetch(1, 0, 256)
+        put(2, 1, 0, S)
+        fetch(1, 256, 512)
+        put(3, 0, 0, S)
+        fetch(2, 0, 256)
+        put(3, 1, 0, S)
+        fetch(2, 256, 512)
+        fetch(3, 0, 256)
+        fetch(3, 256, 384)
+        fetch(3, 384, 512)

@@ -40,49 +40,52 @@ def tile_picked_dwlipagtwo_none_p_kernel(
             nc.sync.dma_start(t[:], src)
             return t
 
-        def load_scales(name, src, row):
-            t = keep.tile([P, TABLE], U8, name=name)
+        def load_scales(name, src, row, queues):
+            t = keep.tile([P, TABLE], U8, name=name, tag=name, align_bytes=64)
             nc.vector.memset(t[:].bitcast(I32), 0)
             for q in range(4):
-                nc.scalar.dma_start(
+                queues[q].dma_start(
                     out=t[32 * q + row : 32 * q + row + 4, :].bitcast(I32),
                     in_=src[0, 4 * q : 4 * q + 4, :].bitcast(I32),
                 )
             return t
 
         def load_words(name, src):
-            t = keep.tile([P, TABLE], U32, name=name)
+            t = keep.tile([P, TABLE], U32, name=name, tag=name, align_bytes=64)
             nc.sync.dma_start(out=t[:].bitcast(I32), in_=src[0].rearrange("p c r -> p (c r)").bitcast(I32))
+            return t
+
+        w_rows = w1.rearrange("(p t) m -> p t m", t=PACK)
+
+        def load_weights(lo, hi, tag):
+            t = keep.tile([P, PACK, hi - lo], F32, name=f"w_raw{lo}", tag=tag, align_bytes=64)
+            nc.sync.dma_start(out=t[:], in_=w_rows[:, :, lo:hi])
             return t
 
         ci_t = load_list("ci_t", ci)
         offs_t = load_list("offs_t", offs)
-        d_scale_table = load_scales("d_scale_table", d_scales, 0)
-        d_word_table = load_words("d_word_table", d_words)
-        x_word_table = load_words("x_word_table", x_words)
-        x_scale_table = load_scales("x_scale_table", x_scales, X_ROW)
-
-        w_rows = w1.rearrange("(p t) m -> p t m", t=PACK)
-        w_first = keep.tile([P, PACK, P], F32)
-        nc.sync.dma_start(out=w_first[:], in_=w_rows[:, :, 0:P])
-        gain = keep.tile([P, PACK], F32)
-        nc.sync.dma_start(out=gain[:], in_=gn.rearrange("(p t) o -> p (t o)", t=PACK))
         n1_t = load_list("n1_t", n1)
         n2_t = load_list("n2_t", n2)
-        w_rest = keep.tile([P, PACK, N - P], F32)
-        nc.sync.dma_start(out=w_rest[:], in_=w_rows[:, :, P:N])
         n3_t = load_list("n3_t", n3)
+        d_scale_table = load_scales("d_scale_table", d_scales, 0, [nc.scalar] * 4)
+        x_scale_table = load_scales("x_scale_table", x_scales, X_ROW, [nc.scalar] * 2 + [nc.gpsimd] * 2)
+        d_word_table = load_words("d_word_table", d_words)
+        x_word_table = load_words("x_word_table", x_words)
+        gain = keep.tile([P, PACK], F32)
+        nc.gpsimd.dma_start(out=gain[:], in_=gn.rearrange("(p t) o -> p (t o)", t=PACK))
 
         d_scale = keep.tile([P, PACK, P], U8, align_bytes=64)
         nc.vector.tensor_copy(d_scale[:].rearrange("p t s -> p s t"), d_scale_table[:].indirect(ci_t[:]))
-        x_scale = keep.tile([P, S], U8, align_bytes=64)
-        nc.vector.tensor_copy(x_scale[:], x_scale_table[:].indirect(offs_t[:]))
+        w_raw0 = load_weights(0, P, "d_scale_table")
         d_code = keep.tile([P, PACK, P], U32, align_bytes=64)
         nc.vector.tensor_copy(d_code[:].rearrange("p t s -> p s t"), d_word_table[:].indirect(ci_t[:]))
+        x_scale = keep.tile([P, S], U8, align_bytes=64)
+        nc.vector.tensor_copy(x_scale[:], x_scale_table[:].indirect(offs_t[:]))
+        w_raw1 = load_weights(P, 2 * P, "d_word_table")
 
         score = []
         for a in range(2):
-            x_code = keep.tile([P, HALF], U32, align_bytes=64, name=f"x_code{a}")
+            x_code = keep.tile([P, HALF], U32, align_bytes=64, name=f"x_code{a}", tag=("x_scale_table", "x_code")[a])
             nc.vector.tensor_copy(x_code[:], x_word_table[:].indirect(offs_t[:, 8 * a : 8 * a + 8]))
             bank = psum.tile([P, PACK, HALF], F32, name=f"score{a}")
             for t in range(PACK):
@@ -97,25 +100,31 @@ def tile_picked_dwlipagtwo_none_p_kernel(
                 )
             score.append(bank)
 
-        def round_weights(b, copy):
-            raw = w_first[:] if b == 0 else w_rest[:, :, (b - 1) * P : b * P]
-            grouped = keep.tile([P, P, PACK], BF16, align_bytes=64, name=f"w_bf{b}")
-            copy(grouped[:].rearrange("p (c i) t -> p c t i", i=4), raw.rearrange("p t (c i) -> p c t i", i=4))
+        w_raw2 = load_weights(2 * P, N, "x_word_table")
+        w_raw = [w_raw0[:], w_raw1[:], w_raw2[:, :, 0:P], w_raw2[:, :, P : 2 * P]]
+
+        def round_on_scalar(dst, src):
+            nc.scalar.activation(dst, src, COPY)
+
+        def round_weights(b, copy, tag):
+            grouped = keep.tile([P, P, PACK], BF16, align_bytes=64, name=f"w_bf{b}", tag=tag)
+            copy(grouped[:].rearrange("p (c i) t -> p c t i", i=4), w_raw[b].rearrange("p t (c i) -> p c t i", i=4))
             return grouped
 
         def quantise_weights(b, grouped):
-            code = keep.tile([P, P], U32, align_bytes=64, name=f"w_code{b}")
+            code = keep.tile([P, P], U32, align_bytes=64, name=f"w_code{b}", tag=f"w_code{b}")
             scale = keep.tile([P, P], U8, align_bytes=64, name=f"w_scale{b}")
             nc.vector.quantize_mx(out=code[:].bitcast(FP8X4), scales=scale[:], in_=grouped[:].rearrange("p c t -> p (c t)"))
             return code, scale
 
-        w_bf0 = round_weights(0, nc.scalar.copy)
+        w_bf0 = round_weights(0, round_on_scalar, "w_bf0")
+        w_bf1 = round_weights(1, round_on_scalar, "w_bf1")
 
         z_code = keep.tile([P, S], U32, align_bytes=64)
         z_scale = keep.tile([P, S], U8, align_bytes=64)
-        z_bf = []
-        for a in range(2):
-            t = keep.tile([P, HALF, PACK], BF16, align_bytes=64, name=f"z_bf{a}")
+
+        def quantise_z(a):
+            t = keep.tile([P, HALF, PACK], BF16, align_bytes=64, name=f"z_bf{a}", tag="z_bf")
             nc.vector.scalar_tensor_tensor(
                 out=t[:],
                 in0=score[a][:].rearrange("p t j -> p j t"),
@@ -124,11 +133,8 @@ def tile_picked_dwlipagtwo_none_p_kernel(
                 op0=MULT,
                 op1=MULT,
             )
-            z_bf.append(t)
-
-        def quantise_z(a):
             cols = slice(a * HALF, (a + 1) * HALF)
-            nc.vector.quantize_mx(out=z_code[:, cols].bitcast(FP8X4), scales=z_scale[:, cols], in_=z_bf[a][:].rearrange("p j t -> p (j t)"))
+            nc.vector.quantize_mx(out=z_code[:, cols].bitcast(FP8X4), scales=z_scale[:, cols], in_=t[:].rearrange("p j t -> p (j t)"))
 
         h_sb = [keep.tile([P, S], F32, name=f"h{b}") for b in range(4)]
         page = [keep.tile([P, U], F32, name=f"page{b}") for b in range(4)]
@@ -156,30 +162,36 @@ def tile_picked_dwlipagtwo_none_p_kernel(
             res = keep.tile([P, hi - lo], F32, name=f"res{b}_{lo}")
             nc.vector.tensor_tensor(res[:], page[b][:, lo:hi], got[:], SUBTRACT)
             nc.sync.dma_start(out=out[b * P : (b + 1) * P, lo:hi], in_=res[:])
+            return got
 
         quantise_z(0)
         w0 = quantise_weights(0, w_bf0)
-        quantise_z(1)
         layer(0, w0, 0, HALF)
+        w1q = quantise_weights(1, w_bf1)
+        layer(1, w1q, 0, HALF)
+        quantise_z(1)
         layer(0, w0, HALF, S)
-        for b in range(1, 4):
-            layer(b, quantise_weights(b, round_weights(b, nc.vector.tensor_copy)), 0, S)
+        layer(1, w1q, HALF, S)
+        layer(2, quantise_weights(2, round_weights(2, nc.vector.tensor_copy, "w_code0")), 0, S)
+        layer(3, quantise_weights(3, round_weights(3, nc.vector.tensor_copy, "w_code1")), 0, S)
 
         put(0, 0, 0, HALF)
+        put(1, 0, 0, HALF)
         put(0, 1, 0, HALF)
+        put(1, 1, 0, HALF)
         put(0, 0, HALF, S)
-        put(1, 0, 0, S)
+        put(1, 0, HALF, S)
         put(0, 1, HALF, S)
-        put(1, 1, 0, S)
-        fetch(0, 0, 256)
-        fetch(0, 256, 512)
+        put(1, 1, HALF, S)
+        g = fetch(0, 0, 256)
         put(2, 0, 0, S)
-        fetch(1, 0, 256)
+        fetch(0, 256, 512)
         put(2, 1, 0, S)
-        fetch(1, 256, 512)
+        fetch(1, 0, 256)
         put(3, 0, 0, S)
-        fetch(2, 0, 256)
+        fetch(1, 256, 512)
         put(3, 1, 0, S)
+        fetch(2, 0, 256)
         fetch(2, 256, 512)
         fetch(3, 0, 256)
         fetch(3, 256, 384)

@@ -62,46 +62,61 @@ def tile_picked_dwlipagtwo_none_p_kernel(
             nc.sync.dma_start(out=t[:], in_=w_rows[:, :, lo:hi])
             return t
 
+        d_scale_stage = keep.tile([P, 2, TABLE], U8)
+        for h in range(2):
+            nc.sync.dma_start(
+                out=d_scale_stage[64 * h : 64 * h + 4, :, :].bitcast(I32),
+                in_=d_scales[0, 8 * h : 8 * h + 8, :].rearrange("(q r) c -> r q c", q=2).bitcast(I32),
+            )
         ci_t = load_list("ci_t", ci)
+        d_word_table = load_words("d_word_table", d_words)
+        x_scale_table = load_scales("x_scale_table", x_scales, X_ROW, [nc.sync] * 4)
         offs_t = load_list("offs_t", offs)
+        x_word_table = load_words("x_word_table", x_words)
+        d_scale_table = keep.tile([P, TABLE], U8)
+        nc.vector.memset(d_scale_table[:].bitcast(I32), 0)
+        for q in range(4):
+            nc.vector.tensor_copy(
+                d_scale_table[32 * q : 32 * q + 4, :].bitcast(I32),
+                d_scale_stage[64 * (q // 2) : 64 * (q // 2) + 4, q % 2, :].bitcast(I32),
+            )
+        w_a = load_weights(0, P, "w_a")
+        gain = keep.tile([P, PACK], F32)
+        nc.sync.dma_start(out=gain[:], in_=gn.rearrange("(p t) o -> p (t o)", t=PACK))
+        w_b = load_weights(P, 2 * P, "w_b")
         n1_t = load_list("n1_t", n1)
         n2_t = load_list("n2_t", n2)
+        w_hi = load_weights(2 * P, N, "w_hi")
         n3_t = load_list("n3_t", n3)
-        d_scale_table = load_scales("d_scale_table", d_scales, 0, [nc.scalar] * 4)
-        x_scale_table = load_scales("x_scale_table", x_scales, X_ROW, [nc.scalar] * 2 + [nc.gpsimd] * 2)
-        d_word_table = load_words("d_word_table", d_words)
-        x_word_table = load_words("x_word_table", x_words)
-        gain = keep.tile([P, PACK], F32)
-        nc.gpsimd.dma_start(out=gain[:], in_=gn.rearrange("(p t) o -> p (t o)", t=PACK))
+        w_raw = [w_a[:], w_b[:], w_hi[:, :, 0:P], w_hi[:, :, P : 2 * P]]
 
         d_scale = keep.tile([P, PACK, P], U8, align_bytes=64)
         nc.vector.tensor_copy(d_scale[:].rearrange("p t s -> p s t"), d_scale_table[:].indirect(ci_t[:]))
-        w_raw0 = load_weights(0, P, "d_scale_table")
         d_code = keep.tile([P, PACK, P], U32, align_bytes=64)
         nc.vector.tensor_copy(d_code[:].rearrange("p t s -> p s t"), d_word_table[:].indirect(ci_t[:]))
+
+        def gather_x(a, tag):
+            x_code = keep.tile([P, HALF], U32, align_bytes=64, name=f"x_code{a}", tag=tag)
+            nc.vector.tensor_copy(x_code[:], x_word_table[:].indirect(offs_t[:, 8 * a : 8 * a + 8]))
+            return x_code
+
         x_scale = keep.tile([P, S], U8, align_bytes=64)
         nc.vector.tensor_copy(x_scale[:], x_scale_table[:].indirect(offs_t[:]))
-        w_raw1 = load_weights(P, 2 * P, "d_word_table")
+        x_code = [gather_x(0, "x_code0"), gather_x(1, "x_code1")]
 
-        score = []
-        for a in range(2):
-            x_code = keep.tile([P, HALF], U32, align_bytes=64, name=f"x_code{a}", tag=("x_scale_table", "x_code")[a])
-            nc.vector.tensor_copy(x_code[:], x_word_table[:].indirect(offs_t[:, 8 * a : 8 * a + 8]))
-            bank = psum.tile([P, PACK, HALF], F32, name=f"score{a}")
+        def scores(a, tag):
+            bank = psum.tile([P, PACK, HALF], F32, name=f"score{a}", tag=tag)
             for t in range(PACK):
                 nc.tensor.matmul_mx(
                     out=bank[:, t, :],
                     lhsT=d_code[:, t, :].bitcast(FP8X4),
                     lhsT_scale=d_scale[:, t, :],
-                    rhs=x_code[:].bitcast(FP8X4),
+                    rhs=x_code[a][:].bitcast(FP8X4),
                     rhs_scale=x_scale[X_ROW:P, a * HALF : (a + 1) * HALF],
                     start=True,
                     stop=True,
                 )
-            score.append(bank)
-
-        w_raw2 = load_weights(2 * P, N, "x_word_table")
-        w_raw = [w_raw0[:], w_raw1[:], w_raw2[:, :, 0:P], w_raw2[:, :, P : 2 * P]]
+            return bank
 
         def round_on_scalar(dst, src):
             nc.scalar.activation(dst, src, COPY)
@@ -111,8 +126,8 @@ def tile_picked_dwlipagtwo_none_p_kernel(
             copy(grouped[:].rearrange("p (c i) t -> p c t i", i=4), w_raw[b].rearrange("p t (c i) -> p c t i", i=4))
             return grouped
 
-        def quantise_weights(b, grouped):
-            code = keep.tile([P, P], U32, align_bytes=64, name=f"w_code{b}", tag=f"w_code{b}")
+        def quantise_weights(b, grouped, tag):
+            code = keep.tile([P, P], U32, align_bytes=64, name=f"w_code{b}", tag=tag)
             scale = keep.tile([P, P], U8, align_bytes=64, name=f"w_scale{b}")
             nc.vector.quantize_mx(out=code[:].bitcast(FP8X4), scales=scale[:], in_=grouped[:].rearrange("p c t -> p (c t)"))
             return code, scale
@@ -123,24 +138,23 @@ def tile_picked_dwlipagtwo_none_p_kernel(
         z_code = keep.tile([P, S], U32, align_bytes=64)
         z_scale = keep.tile([P, S], U8, align_bytes=64)
 
-        def quantise_z(a):
-            t = keep.tile([P, HALF, PACK], BF16, align_bytes=64, name=f"z_bf{a}", tag="z_bf")
+        def quantise_z(lo, hi, bank, tag):
+            t = keep.tile([P, hi - lo, PACK], BF16, align_bytes=64, name=f"z_bf{lo}", tag=tag)
             nc.vector.scalar_tensor_tensor(
                 out=t[:],
-                in0=score[a][:].rearrange("p t j -> p j t"),
+                in0=bank[:, :, lo % HALF : lo % HALF + hi - lo].rearrange("p t j -> p j t"),
                 scalar=0.0625,
-                in1=gain[:].unsqueeze(1).to_broadcast([P, HALF, PACK]),
+                in1=gain[:].unsqueeze(1).to_broadcast([P, hi - lo, PACK]),
                 op0=MULT,
                 op1=MULT,
             )
-            cols = slice(a * HALF, (a + 1) * HALF)
-            nc.vector.quantize_mx(out=z_code[:, cols].bitcast(FP8X4), scales=z_scale[:, cols], in_=t[:].rearrange("p j t -> p (j t)"))
+            nc.vector.quantize_mx(out=z_code[:, lo:hi].bitcast(FP8X4), scales=z_scale[:, lo:hi], in_=t[:].rearrange("p j t -> p (j t)"))
 
         h_sb = [keep.tile([P, S], F32, name=f"h{b}") for b in range(4)]
         page = [keep.tile([P, U], F32, name=f"page{b}") for b in range(4)]
 
-        def layer(b, w, lo, hi):
-            bank = psum.tile([P, hi - lo], F32, name=f"h_bank{b}_{lo}")
+        def layer(b, w, lo, hi, tag):
+            bank = psum.tile([P, hi - lo], F32, name=f"h_bank{b}_{lo}", tag=tag)
             nc.tensor.matmul_mx(
                 out=bank[:],
                 lhsT=w[0][:].bitcast(FP8X4),
@@ -164,25 +178,25 @@ def tile_picked_dwlipagtwo_none_p_kernel(
             nc.sync.dma_start(out=out[b * P : (b + 1) * P, lo:hi], in_=res[:])
             return got
 
-        quantise_z(0)
-        w0 = quantise_weights(0, w_bf0)
-        layer(0, w0, 0, HALF)
-        w1q = quantise_weights(1, w_bf1)
-        layer(1, w1q, 0, HALF)
-        quantise_z(1)
-        layer(0, w0, HALF, S)
-        layer(1, w1q, HALF, S)
-        layer(2, quantise_weights(2, round_weights(2, nc.vector.tensor_copy, "w_code0")), 0, S)
-        layer(3, quantise_weights(3, round_weights(3, nc.vector.tensor_copy, "w_code1")), 0, S)
+        w0 = quantise_weights(0, w_bf0, "w_code0")
+        first = scores(0, "bank0")
+        quantise_z(0, 64, first, "z_bf0")
+        layer(0, w0, 0, 64, "bank1")
+        w1q = quantise_weights(1, w_bf1, "z_bf0")
+        layer(1, w1q, 0, 64, "bank2")
+        quantise_z(64, HALF, first, "z_bf1")
+        layer(0, w0, 64, HALF, "bank3")
+        layer(1, w1q, 64, HALF, "bank4")
+        quantise_z(HALF, S, scores(1, "bank1"), "z_bf2")
+        layer(0, w0, HALF, S, "bank5")
+        layer(1, w1q, HALF, S, "bank6")
+        layer(2, quantise_weights(2, round_weights(2, nc.vector.tensor_copy, "w_code0"), "w_code2"), 0, S, "bank7")
+        layer(3, quantise_weights(3, round_weights(3, nc.vector.tensor_copy, "z_bf0"), "w_code3"), 0, S, "bank0")
 
-        put(0, 0, 0, HALF)
-        put(1, 0, 0, HALF)
-        put(0, 1, 0, HALF)
-        put(1, 1, 0, HALF)
-        put(0, 0, HALF, S)
-        put(1, 0, HALF, S)
-        put(0, 1, HALF, S)
-        put(1, 1, HALF, S)
+        for lo, hi in ((0, 64), (64, HALF), (HALF, S)):
+            for which in range(2):
+                for b in range(2):
+                    put(b, which, lo, hi)
         g = fetch(0, 0, 256)
         put(2, 0, 0, S)
         fetch(0, 256, 512)

from contextlib import ExitStack

import concourse.mybir as mybir

F32 = mybir.dt.float32
BF16 = mybir.dt.bfloat16
I32 = mybir.dt.int32
U32 = mybir.dt.uint32
U16 = mybir.dt.uint16
U8 = mybir.dt.uint8
FP8X4 = mybir.dt.float8_e4m3fn_x4
MULT = mybir.AluOpType.mult
SUBTRACT = mybir.AluOpType.subtract
COPY = mybir.ActivationFunctionType.Copy

P = 128
PACK = 4
TABLE = 2048
S = 256
H = 512
N = 512
U = 512
HALF = S // 2
X_ROW = 4

FLOPS = 2 * 512 * H * S + 2 * H * N * S


def tile_picked_dwlipagtwo_none_p_kernel(
    tc, x_words, x_scales, d_words, d_scales, gn, w1, offs, ci, n1, n2, n3, out
):
    nc = tc.nc
    with ExitStack() as ctx:
        lists = ctx.enter_context(tc.tile_pool(name="lists", bufs=1))
        keep = ctx.enter_context(tc.tile_pool(name="keep", bufs=1))
        psum = ctx.enter_context(tc.psum_pool(name="psum", bufs=1))

        def load_list(name, src):
            t = lists.tile([P, src.shape[1]], U16, name=name)
            nc.sync.dma_start(t[:], src)
            return t

        def load_scales(name, src, row, queues):
            t = keep.tile([P, TABLE], U8, name=name, tag=name, align_bytes=64)
            nc.vector.memset(t[:].bitcast(I32), 0)
            for q in range(4):
                queues[q].dma_start(
                    out=t[32 * q + row : 32 * q + row + 4, :].bitcast(I32),
                    in_=src[0, 4 * q : 4 * q + 4, :].bitcast(I32),
                )
            return t

        def load_words(name, src):
            t = keep.tile([P, TABLE], U32, name=name, tag=name, align_bytes=64)
            nc.sync.dma_start(out=t[:].bitcast(I32), in_=src[0].rearrange("p c r -> p (c r)").bitcast(I32))
            return t

        w_rows = w1.rearrange("(p t) m -> p t m", t=PACK)

        def load_weights(lo, hi, tag):
            t = keep.tile([P, PACK, hi - lo], F32, name=f"w_raw{lo}", tag=tag, align_bytes=64)
            nc.sync.dma_start(out=t[:], in_=w_rows[:, :, lo:hi])
            return t

        d_scale_stage = keep.tile([P, 2, TABLE], U8)
        for h in range(2):
            nc.sync.dma_start(
                out=d_scale_stage[64 * h : 64 * h + 4, :, :].bitcast(I32),
                in_=d_scales[0, 8 * h : 8 * h + 8, :].rearrange("(q r) c -> r q c", q=2).bitcast(I32),
            )
        ci_t = load_list("ci_t", ci)
        d_word_table = load_words("d_word_table", d_words)
        x_scale_table = load_scales("x_scale_table", x_scales, X_ROW, [nc.sync] * 4)
        offs_t = load_list("offs_t", offs)
        x_word_table = load_words("x_word_table", x_words)
        d_scale_table = keep.tile([P, TABLE], U8)
        nc.vector.memset(d_scale_table[:].bitcast(I32), 0)
        for q in range(4):
            nc.vector.tensor_copy(
                d_scale_table[32 * q : 32 * q + 4, :].bitcast(I32),
                d_scale_stage[64 * (q // 2) : 64 * (q // 2) + 4, q % 2, :].bitcast(I32),
            )
        w_a = load_weights(0, P, "w_a")
        gain = keep.tile([P, PACK], F32)
        nc.sync.dma_start(out=gain[:], in_=gn.rearrange("(p t) o -> p (t o)", t=PACK))
        w_b = load_weights(P, 2 * P, "w_b")
        n1_t = load_list("n1_t", n1)
        n2_t = load_list("n2_t", n2)
        w_hi = load_weights(2 * P, N, "w_hi")
        n3_t = load_list("n3_t", n3)
        w_raw = [w_a[:], w_b[:], w_hi[:, :, 0:P], w_hi[:, :, P : 2 * P]]

        d_scale = keep.tile([P, PACK, P], U8, align_bytes=64)
        nc.vector.tensor_copy(d_scale[:].rearrange("p t s -> p s t"), d_scale_table[:].indirect(ci_t[:]))
        d_code = keep.tile([P, PACK, P], U32, align_bytes=64)
        nc.vector.tensor_copy(d_code[:].rearrange("p t s -> p s t"), d_word_table[:].indirect(ci_t[:]))

        def gather_x(a, tag):
            x_code = keep.tile([P, HALF], U32, align_bytes=64, name=f"x_code{a}", tag=tag)
            nc.vector.tensor_copy(x_code[:], x_word_table[:].indirect(offs_t[:, 8 * a : 8 * a + 8]))
            return x_code

        x_scale = keep.tile([P, S], U8, align_bytes=64)
        nc.vector.tensor_copy(x_scale[:], x_scale_table[:].indirect(offs_t[:]))
        x_code = [gather_x(0, "x_code0"), gather_x(1, "x_code1")]

        def scores(a, tag):
            bank = psum.tile([P, PACK, HALF], F32, name=f"score{a}", tag=tag)
            for t in range(PACK):
                nc.tensor.matmul_mx(
                    out=bank[:, t, :],
                    lhsT=d_code[:, t, :].bitcast(FP8X4),
                    lhsT_scale=d_scale[:, t, :],
                    rhs=x_code[a][:].bitcast(FP8X4),
                    rhs_scale=x_scale[X_ROW:P, a * HALF : (a + 1) * HALF],
                    start=True,
                    stop=True,
                )
            return bank

        def round_on_scalar(dst, src):
            nc.scalar.activation(dst, src, COPY)

        def round_weights(b, copy, tag):
            grouped = keep.tile([P, P, PACK], BF16, align_bytes=64, name=f"w_bf{b}", tag=tag)
            copy(grouped[:].rearrange("p (c i) t -> p c t i", i=4), w_raw[b].rearrange("p t (c i) -> p c t i", i=4))
            return grouped

        def quantise_weights(b, grouped, tag):
            code = keep.tile([P, P], U32, align_bytes=64, name=f"w_code{b}", tag=tag)
            scale = keep.tile([P, P], U8, align_bytes=64, name=f"w_scale{b}")
            nc.vector.quantize_mx(out=code[:].bitcast(FP8X4), scales=scale[:], in_=grouped[:].rearrange("p c t -> p (c t)"))
            return code, scale

        w_bf0 = round_weights(0, round_on_scalar, "w_bf0")
        w_bf1 = round_weights(1, round_on_scalar, "w_bf1")

        z_code = keep.tile([P, S], U32, align_bytes=64)
        z_scale = keep.tile([P, S], U8, align_bytes=64)

        def quantise_z(lo, hi, bank, tag):
            t = keep.tile([P, hi - lo, PACK], BF16, align_bytes=64, name=f"z_bf{lo}", tag=tag)
            nc.vector.scalar_tensor_tensor(
                out=t[:],
                in0=bank[:, :, lo % HALF : lo % HALF + hi - lo].rearrange("p t j -> p j t"),
                scalar=0.0625,
                in1=gain[:].unsqueeze(1).to_broadcast([P, hi - lo, PACK]),
                op0=MULT,
                op1=MULT,
            )
            nc.vector.quantize_mx(out=z_code[:, lo:hi].bitcast(FP8X4), scales=z_scale[:, lo:hi], in_=t[:].rearrange("p j t -> p (j t)"))

        h_sb = [keep.tile([P, S], F32, name=f"h{b}") for b in range(4)]
        page = [keep.tile([P, U], F32, name=f"page{b}") for b in range(4)]

        def layer(b, w, lo, hi, tag):
            bank = psum.tile([P, hi - lo], F32, name=f"h_bank{b}_{lo}", tag=tag)
            nc.tensor.matmul_mx(
                out=bank[:],
                lhsT=w[0][:].bitcast(FP8X4),
                lhsT_scale=w[1][:],
                rhs=z_code[:, lo:hi].bitcast(FP8X4),
                rhs_scale=z_scale[:, lo:hi],
                start=True,
                stop=True,
            )
            nc.vector.tensor_copy(h_sb[b][:, lo:hi], bank[:])

        def put(b, which, lo, hi):
            idx, factor = ((n1_t, 1.0), (n2_t, 0.5))[which]
            nc.scalar.activation(page[b][:].indirect(idx[:, lo // 16 : hi // 16]), h_sb[b][:, lo:hi], COPY, scale=factor)

        def fetch(b, lo, hi):
            got = keep.tile([P, hi - lo], F32, name=f"got{b}_{lo}")
            nc.scalar.activation(got[:], page[b][:].indirect(n3_t[:, lo // 16 : hi // 16]), COPY)
            res = keep.tile([P, hi - lo], F32, name=f"res{b}_{lo}")
            nc.vector.tensor_tensor(res[:], page[b][:, lo:hi], got[:], SUBTRACT)
            nc.sync.dma_start(out=out[b * P : (b + 1) * P, lo:hi], in_=res[:])
            return got

        w0 = quantise_weights(0, w_bf0, "w_code0")
        first = scores(0, "bank0")
        quantise_z(0, 64, first, "z_bf0")
        layer(0, w0, 0, 64, "bank1")
        w1q = quantise_weights(1, w_bf1, "z_bf0")
        layer(1, w1q, 0, 64, "bank2")
        quantise_z(64, HALF, first, "z_bf1")
        layer(0, w0, 64, HALF, "bank3")
        layer(1, w1q, 64, HALF, "bank4")
        quantise_z(HALF, S, scores(1, "bank1"), "z_bf2")
        layer(0, w0, HALF, S, "bank5")
        layer(1, w1q, HALF, S, "bank6")
        layer(2, quantise_weights(2, round_weights(2, nc.vector.tensor_copy, "w_code0"), "w_code2"), 0, S, "bank7")
        layer(3, quantise_weights(3, round_weights(3, nc.vector.tensor_copy, "z_bf0"), "w_code3"), 0, S, "bank0")

        for lo, hi in ((0, 64), (64, HALF), (HALF, S)):
            for which in range(2):
                for b in range(2):
                    put(b, which, lo, hi)
        g = fetch(0, 0, 256)
        put(2, 0, 0, S)
        fetch(0, 256, 512)
        put(2, 1, 0, S)
        fetch(1, 0, 256)
        put(3, 0, 0, S)
        fetch(1, 256, 512)
        put(3, 1, 0, S)
        fetch(2, 0, 256)
        fetch(2, 256, 512)
        fetch(3, 0, 256)
        fetch(3, 256, 384)
        fetch(3, 384, 512)
